import numpy as np
import ml_dtypes


def mxq(x, axis, fmt="e4m3"):
    dtype, down = {"e4m3": (ml_dtypes.float8_e4m3fn, 7), "e5m2": (ml_dtypes.float8_e5m2, 14)}[fmt]
    v = np.moveaxis(np.asarray(x, np.float32).astype(ml_dtypes.bfloat16).astype(np.float64), axis, -1)
    blocks = v.reshape(v.shape[:-1] + (-1, 32))
    amax = np.abs(blocks).max(-1, keepdims=True)
    byte = np.maximum(np.where(amax > 0, np.frexp(amax)[1] - 1 + 127, 0) - down, 1)
    scale = np.exp2(byte - 127.0)
    codes = (blocks / scale).astype(np.float32).astype(dtype).astype(np.float64)
    return np.moveaxis((codes * scale).reshape(v.shape), -1, axis)


WIDE = False


def mx_kscale(k):
    if not WIDE:
        return np.ones(k)
    levels = np.array([10, -10, 5, -5, 0])
    if k % 512:
        return np.exp2(np.random.permutation(np.resize(levels, k // 32))).repeat(32)
    a = np.empty((k // 512, 16))
    for p in range(k // 512):
        a[p, :8] = np.random.permutation(np.resize(levels, 8))
        for g in range(8):
            far = levels[np.abs(levels - a[p, g]) >= 10]
            a[p, g + 8] = far[np.random.randint(len(far))]
    return np.exp2(a.ravel()).repeat(32)


def f64(x):
    return np.asarray(x).astype(np.float64)


def striped(idx):
    return np.tile(np.asarray(idx).reshape(-1, 16).T, (8, 1)).astype(np.uint16)


def unstriped(offs):
    return offs[:16].T.reshape(-1).astype(np.int64)


def striped8(idx):
    return np.asarray(idx).reshape(8, -1, 16).transpose(0, 2, 1).reshape(128, -1).astype(np.uint16)


def unstriped8(offs):
    return offs.reshape(8, 16, -1).transpose(0, 2, 1).reshape(8, -1).astype(np.int64)


def pick8(x, idx, run):
    r = np.arange(len(x))
    return x[r[:, None], idx[r % (8 * run) // run]]


E2M1 = np.array([0.0, 0.5, 1.0, 1.5, 2.0, 3.0, 4.0, 6.0, -0.0, -0.5, -1.0, -1.5, -2.0, -3.0, -4.0, -6.0])


def pack_weight(w, fmt):
    k, n = w.shape
    w = f64(np.asarray(w, np.float32).astype(ml_dtypes.bfloat16)).reshape(k // 32, 32, n)
    amax = np.abs(w).max(1)
    if fmt == "e4m3":
        byte = np.frexp(amax)[1] - 1 + 127 - 7
    else:
        mant, ex = np.frexp(amax / 6.0)
        byte = np.where(mant > 0.5, ex, ex - 1) + 127
    byte = np.clip(np.where(amax > 0, byte, 1), 1, 254)
    scaled = (w * np.exp2(127.0 - byte)[:, None, :]).reshape(k, n).astype(np.float32)
    by_word = np.ascontiguousarray(scaled.reshape(k // 512, 128, 4, n).transpose(0, 1, 3, 2))
    if fmt == "e4m3":
        words = by_word.astype(ml_dtypes.float8_e4m3fn).view(np.uint8)
    else:
        c = by_word.astype(ml_dtypes.float4_e2m1fn).view(np.uint8) & 0xF
        words = (c[..., 0::2] | (c[..., 1::2] << 4)).reshape(k // 512, 128, 2 * n)
    return np.ascontiguousarray(words), np.ascontiguousarray(byte.astype(np.uint8).reshape(k // 512, 16, n))


def unpack_weight(words, scales, fmt):
    g, _, n = scales.shape
    words = np.ascontiguousarray(words).reshape(g, 128, n, -1)
    if fmt == "e4m3":
        vals = words.view(ml_dtypes.float8_e4m3fn).astype(np.float64)
    else:
        nib = np.empty((g, 128, n, 4), np.uint8)
        nib[..., 0::2] = words & 0xF
        nib[..., 1::2] = words >> 4
        vals = E2M1[nib]
    vals = vals * np.repeat(np.exp2(scales.astype(np.float64) - 127.0), 8, axis=1)[..., None]
    return vals.transpose(0, 1, 3, 2).reshape(g * 512, n)


def sigmoid(v):
    return 1.0 / (1.0 + np.exp(-v))


K, R, F, T, J, U, M = 512, 128, 512, 2048, 512, 1024, 256


def setup_inputs():
    n = np.random.standard_normal
    idx = np.random.permutation(T)[:J]
    idx2 = np.random.permutation(U)[:J]
    idx3 = np.stack([np.random.permutation(J)[:M] for _ in range(8)])
    fk = mx_kscale(K)
    ff = mx_kscale(F)
    tabp = pack_weight(n((K, T)) / fk[:, None], "e4m3")
    return {
        "tab_words": tabp[0],
        "tab_scales": tabp[1],
        "w1": (n((K, R)) * 1 / np.sqrt(K) * fk[:, None]).astype(np.float32),
        "lift": (n((R, U)) * 0.5).astype(np.float32),
        "wo": (n((F, R)) * 1 / np.sqrt(F) * ff[:, None]).astype(np.float32),
        "dy": (n((F, M)) / ff[:, None]).astype(np.float32),
        "old": (0.5 * n((R, J))).astype(np.float32),
        "offs": striped(idx),
        "offs2": striped(idx2),
        "offs3": striped8(idx3),
    }


def reference(tab_words, tab_scales, w1, lift, wo, dy, old, offs, offs2, offs3):
    idx = unstriped(offs)
    idx2 = unstriped(offs2)
    idx3 = unstriped8(offs3)
    tabu = unpack_weight(tab_words, tab_scales, "e4m3")
    w1q = mxq(f64(w1), 0, "e4m3")
    tabidxg = tabu[:, idx]
    a = w1q.T @ tabidxg
    h1 = np.tanh(a)
    h2 = h1 * np.exp(f64(lift)[:, idx2])
    woq = mxq(f64(wo), 0, "e4m3")
    dyq = mxq(f64(dy), 0, "e4m3")
    c0 = woq.T @ dyq
    e1 = c0 * sigmoid(pick8(h2, idx3, 16)) * (1.0 + pick8(h2, idx3, 16) * (1.0 - sigmoid(pick8(h2, idx3, 16))))
    s1 = np.zeros((R, J))
    s1[np.arange(R)[:, None], idx3[np.arange(R) % 128 // 16]] = e1
    dh1 = s1 * np.exp(f64(lift)[:, idx2])
    da = dh1 * (1.0 - np.square(h1))
    y = da + f64(old)
    return y

@@ -1,0 +1,152 @@
+from contextlib import ExitStack
+
+import concourse.mybir as mybir
+
+F32 = mybir.dt.float32
+BF16 = mybir.dt.bfloat16
+I32 = mybir.dt.int32
+U32 = mybir.dt.uint32
+U16 = mybir.dt.uint16
+U8 = mybir.dt.uint8
+FP8X4 = mybir.dt.float8_e4m3fn_x4
+ACT = mybir.ActivationFunctionType
+ALU = mybir.AluOpType
+
+P = 128
+PACK = 4
+K, R, F, T, J, U, M = 512, 128, 512, 2048, 512, 1024, 256
+HALF = J // 2
+LIFT_WINDOW = 2048
+
+FLOPS = 2 * K * R * J + 2 * F * R * M
+
+
+def quantize(nc, codes, scales, grouped):
+    nc.vector.quantize_mx(out=codes[:].bitcast(FP8X4), scales=scales[:], in_=grouped[:].rearrange("p c t -> p (c t)"))
+
+
+def interleave(copy, grouped, raw):
+    copy(
+        out=grouped.rearrange("p (c i) t -> p c t i", i=4),
+        in_=raw.rearrange("p t (c i) -> p c t i", i=4),
+    )
+
+
+def tile_attend_cliftedpicks_kernel(tc, tab_words, tab_scales, w1, lift, wo, dy, old, offs, offs2, offs3, out):
+    nc = tc.nc
+    with ExitStack() as ctx:
+        sb = ctx.enter_context(tc.tile_pool(name="sb", bufs=1))
+        ps = ctx.enter_context(tc.psum_pool(name="ps", bufs=1))
+
+        tab_list = sb.tile([P, J // 16], U16)
+        lift_list = sb.tile([P, J // 16], U16)
+        pick_lists = sb.tile([P, M // 16], U16)
+        scale_table = sb.tile([P, T], U8, align_bytes=64)
+        lift_table = sb.tile([P, LIFT_WINDOW], F32)
+        word_table = sb.tile([P, T], I32, align_bytes=64)
+        w1_raw = sb.tile([P, PACK, R], F32)
+        wo_raw = sb.tile([P, PACK, R], F32)
+        dy_raw = sb.tile([P, PACK, M], F32)
+        old_sb = sb.tile([P, J], F32)
+        s1 = sb.tile([P, J], F32)
+        minus_one = sb.tile([P, 1], F32)
+
+        nc.vector.memset(scale_table[:].bitcast(I32), 0)
+        for q in range(4):
+            nc.scalar.dma_start(scale_table[32 * q : 32 * q + 4, :].bitcast(I32), tab_scales[0, 4 * q : 4 * q + 4, :].bitcast(I32))
+        nc.sync.dma_start(lift_list[:], offs2)
+        nc.sync.dma_start(tab_list[:], offs)
+        nc.sync.dma_start(lift_table[:, 0:U], lift)
+        nc.sync.dma_start(w1_raw[:], w1.rearrange("(p t) r -> p t r", t=PACK))
+        nc.sync.dma_start(word_table[:], tab_words[0].rearrange("p n t -> p (n t)").bitcast(I32))
+        nc.sync.dma_start(dy_raw[:], dy.rearrange("(p t) m -> p t m", t=PACK))
+        nc.sync.dma_start(wo_raw[:], wo.rearrange("(p t) r -> p t r", t=PACK))
+        nc.sync.dma_start(pick_lists[:], offs3)
+        nc.sync.dma_start(old_sb[:], old)
+
+        nc.vector.memset(minus_one[:], -1.0)
+        warm = sb.tile([P, 1], F32)
+        nc.scalar.activation(warm[:], minus_one[:], ACT.Exp)
+        nc.vector.memset(lift_table[:, U:LIFT_WINDOW], 0.0)
+        nc.vector.memset(s1[:], 0.0)
+
+        e_lift = sb.tile([P, J], F32)
+        e_lift2 = sb.tile([P, J], F32)
+        nc.scalar.activation(e_lift[:], lift_table[:].indirect(lift_list[:]), ACT.Exp)
+
+        tab_sc = sb.tile([P, J], U8, align_bytes=64)
+        nc.vector.tensor_copy(tab_sc[:], scale_table[:].indirect(tab_list[:]))
+
+        w1_bf = sb.tile([P, R, PACK], BF16, align_bytes=64)
+        wo_bf = sb.tile([P, R, PACK], BF16, align_bytes=64)
+        dy_bf = sb.tile([P, M, PACK], BF16, align_bytes=64)
+        w1_codes = sb.tile([P, R], U32, align_bytes=64)
+        w1_sc = sb.tile([P, R], U8, align_bytes=64)
+        wo_codes = sb.tile([P, R], U32, align_bytes=64)
+        wo_sc = sb.tile([P, R], U8, align_bytes=64)
+        dy_codes = sb.tile([P, M], U32, align_bytes=64)
+        dy_sc = sb.tile([P, M], U8, align_bytes=64)
+        interleave(nc.vector.tensor_copy, w1_bf[:], w1_raw[:])
+        quantize(nc, w1_codes, w1_sc, w1_bf)
+        nc.vector.tensor_scalar(e_lift2[:], e_lift[:], 2.0, None, ALU.mult)
+
+        h2 = sb.tile([P, J], F32)
+        sig2a = sb.tile([P, J], F32)
+        h1_sq = sb.tile([P, J], F32)
+        slope_neg = sb.tile([P, J], F32)
+        halves = [slice(0, HALF), slice(HALF, J)]
+        a_ps = []
+        for h in range(2):
+            words = sb.tile([P, HALF], U32, align_bytes=64, name="words%d" % h)
+            nc.vector.tensor_copy(words[:], word_table[:].bitcast(U32).indirect(tab_list[:, 16 * h : 16 * (h + 1)]))
+            bank = ps.tile([P, HALF], F32, name="a%d" % h)
+            nc.tensor.matmul_mx(
+                out=bank[:], lhsT=w1_codes[:].bitcast(FP8X4), lhsT_scale=w1_sc[:],
+                rhs=words[:].bitcast(FP8X4), rhs_scale=tab_sc[:, halves[h]], start=True, stop=True,
+            )
+            a_ps.append(bank)
+
+        interleave(nc.vector.tensor_copy, dy_bf[:], dy_raw[:])
+        quantize(nc, dy_codes, dy_sc, dy_bf)
+
+        for h in range(2):
+            nc.scalar.activation(sig2a[:, halves[h]], a_ps[h][:], ACT.Sigmoid, scale=2.0)
+        for c in halves:
+            nc.vector.scalar_tensor_tensor(h2[:, c], sig2a[:, c], 0.5, e_lift2[:, c], ALU.subtract, ALU.mult)
+
+        interleave(nc.scalar.copy, wo_bf[:], wo_raw[:])
+        quantize(nc, wo_codes, wo_sc, wo_bf)
+        c0_ps = ps.tile([P, M], F32)
+        nc.tensor.matmul_mx(
+            out=c0_ps[:], lhsT=wo_codes[:].bitcast(FP8X4), lhsT_scale=wo_sc[:],
+            rhs=dy_codes[:].bitcast(FP8X4), rhs_scale=dy_sc[:], start=True, stop=True,
+        )
+
+        x = sb.tile([P, M], F32)
+        s = sb.tile([P, M], F32)
+        v = sb.tile([P, M], F32)
+        p = sb.tile([P, M], F32)
+        w = sb.tile([P, M], F32)
+        picks = [slice(0, M // 2), slice(M // 2, M)]
+        for h in range(2):
+            lists = pick_lists[:, 8 * h : 8 * (h + 1)]
+            nc.scalar.activation(s[:, picks[h]], h2[:].indirect(lists), ACT.Sigmoid)
+            nc.vector.tensor_copy(x[:, picks[h]], h2[:].indirect(lists))
+        for c in picks:
+            nc.vector.scalar_tensor_tensor(v[:, c], s[:, c], 1.0, x[:, c], ALU.subtract, ALU.mult)
+        nc.vector.tensor_tensor(p[:], s[:], c0_ps[:], ALU.mult)
+        nc.vector.tensor_scalar(w[:], v[:], -1.0, 1.0, ALU.mult, ALU.add)
+        nc.vector.tensor_tensor(s1[:].indirect(pick_lists[:]), p[:], w[:], ALU.mult)
+
+        for c in halves:
+            nc.scalar.activation(h1_sq[:, c], sig2a[:, c], ACT.Square, scale=2.0, bias=minus_one[:])
+        for c in halves:
+            nc.vector.scalar_tensor_tensor(slope_neg[:, c], h1_sq[:, c], 1.0, e_lift[:, c], ALU.subtract, ALU.mult)
+
+        da_neg = sb.tile([P, J], F32)
+        y = sb.tile([P, J], F32)
+        for c in halves:
+            nc.vector.tensor_tensor(da_neg[:, c], s1[:, c], slope_neg[:, c], ALU.mult)
+        for c in halves:
+            nc.vector.tensor_tensor(y[:, c], old_sb[:, c], da_neg[:, c], ALU.subtract)
+            nc.sync.dma_start(out[:, c], y[:, c])

@@ -55,8 +55,8 @@ def tile_attend_cliftedpicks_kernel(tc, tab_words, tab_scales, w1, lift, wo, dy,
         for q in range(4):
             nc.scalar.dma_start(scale_table[32 * q : 32 * q + 4, :].bitcast(I32), tab_scales[0, 4 * q : 4 * q + 4, :].bitcast(I32))
         nc.sync.dma_start(lift_list[:], offs2)
-        nc.sync.dma_start(tab_list[:], offs)
         nc.sync.dma_start(lift_table[:, 0:U], lift)
+        nc.sync.dma_start(tab_list[:], offs)
         nc.sync.dma_start(w1_raw[:], w1.rearrange("(p t) r -> p t r", t=PACK))
         nc.sync.dma_start(word_table[:], tab_words[0].rearrange("p n t -> p (n t)").bitcast(I32))
         nc.sync.dma_start(dy_raw[:], dy.rearrange("(p t) m -> p t m", t=PACK))
@@ -90,10 +90,8 @@ def tile_attend_cliftedpicks_kernel(tc, tab_words, tab_scales, w1, lift, wo, dy,
         quantize(nc, w1_codes, w1_sc, w1_bf)
         nc.vector.tensor_scalar(e_lift2[:], e_lift[:], 2.0, None, ALU.mult)
 
-        h2 = sb.tile([P, J], F32)
+        h2 = sb.tile([P, J], F32, tag="h2")
         sig2a = sb.tile([P, J], F32)
-        h1_sq = sb.tile([P, J], F32)
-        slope_neg = sb.tile([P, J], F32)
         halves = [slice(0, HALF), slice(HALF, J)]
         a_ps = []
         for h in range(2):
@@ -106,15 +104,17 @@ def tile_attend_cliftedpicks_kernel(tc, tab_words, tab_scales, w1, lift, wo, dy,
             )
             a_ps.append(bank)
 
-        interleave(nc.vector.tensor_copy, dy_bf[:], dy_raw[:])
-        quantize(nc, dy_codes, dy_sc, dy_bf)
-
-        for h in range(2):
-            nc.scalar.activation(sig2a[:, halves[h]], a_ps[h][:], ACT.Sigmoid, scale=2.0)
-        for c in halves:
+        def lifted(h):
+            c = halves[h]
+            nc.scalar.activation(sig2a[:, c], a_ps[h][:], ACT.Sigmoid, scale=2.0)
             nc.vector.scalar_tensor_tensor(h2[:, c], sig2a[:, c], 0.5, e_lift2[:, c], ALU.subtract, ALU.mult)
 
-        interleave(nc.scalar.copy, wo_bf[:], wo_raw[:])
+        interleave(nc.vector.tensor_copy, dy_bf[:], dy_raw[:])
+        lifted(0)
+        quantize(nc, dy_codes, dy_sc, dy_bf)
+        interleave(nc.scalar.copy, wo_bf[:, 0 : R // 2, :], wo_raw[:, :, 0 : R // 2])
+        lifted(1)
+        interleave(nc.scalar.copy, wo_bf[:, R // 2 : R, :], wo_raw[:, :, R // 2 : R])
         quantize(nc, wo_codes, wo_sc, wo_bf)
         c0_ps = ps.tile([P, M], F32)
         nc.tensor.matmul_mx(
@@ -125,23 +125,27 @@ def tile_attend_cliftedpicks_kernel(tc, tab_words, tab_scales, w1, lift, wo, dy,
         x = sb.tile([P, M], F32)
         s = sb.tile([P, M], F32)
         v = sb.tile([P, M], F32)
-        p = sb.tile([P, M], F32)
-        w = sb.tile([P, M], F32)
+        d = sb.tile([P, M], F32)
         picks = [slice(0, M // 2), slice(M // 2, M)]
         for h in range(2):
             lists = pick_lists[:, 8 * h : 8 * (h + 1)]
             nc.scalar.activation(s[:, picks[h]], h2[:].indirect(lists), ACT.Sigmoid)
             nc.vector.tensor_copy(x[:, picks[h]], h2[:].indirect(lists))
+        late = sb.tile([P, M + HALF], F32, tag="h2")
+        c0_neg = late[:, 0:M]
+        nc.scalar.activation(c0_neg, c0_ps[:], ACT.Copy, scale=-1.0)
         for c in picks:
             nc.vector.scalar_tensor_tensor(v[:, c], s[:, c], 1.0, x[:, c], ALU.subtract, ALU.mult)
-        nc.vector.tensor_tensor(p[:], s[:], c0_ps[:], ALU.mult)
-        nc.vector.tensor_scalar(w[:], v[:], -1.0, 1.0, ALU.mult, ALU.add)
-        nc.vector.tensor_tensor(s1[:].indirect(pick_lists[:]), p[:], w[:], ALU.mult)
+        for c in picks:
+            nc.vector.scalar_tensor_tensor(d[:, c], v[:, c], 1.0, s[:, c], ALU.subtract, ALU.mult)
+        nc.vector.tensor_tensor(s1[:].indirect(pick_lists[:]), d[:], c0_neg, ALU.mult)
 
-        for c in halves:
-            nc.scalar.activation(h1_sq[:, c], sig2a[:, c], ACT.Square, scale=2.0, bias=minus_one[:])
-        for c in halves:
-            nc.vector.scalar_tensor_tensor(slope_neg[:, c], h1_sq[:, c], 1.0, e_lift[:, c], ALU.subtract, ALU.mult)
+        h1_sq0 = sb.tile([P, HALF], F32)
+        h1_sq = [h1_sq0[:], late[:, M : M + HALF]]
+        slope_neg = sb.tile([P, J], F32)
+        for h, c in enumerate(halves):
+            nc.scalar.activation(h1_sq[h], sig2a[:, c], ACT.Square, scale=2.0, bias=minus_one[:])
+            nc.vector.scalar_tensor_tensor(slope_neg[:, c], h1_sq[h], 1.0, e_lift[:, c], ALU.subtract, ALU.mult)
 
         da_neg = sb.tile([P, J], F32)
         y = sb.tile([P, J], F32)

@@ -55,8 +55,8 @@ def tile_attend_cliftedpicks_kernel(tc, tab_words, tab_scales, w1, lift, wo, dy,
         for q in range(4):
             nc.scalar.dma_start(scale_table[32 * q : 32 * q + 4, :].bitcast(I32), tab_scales[0, 4 * q : 4 * q + 4, :].bitcast(I32))
         nc.sync.dma_start(lift_list[:], offs2)
-        nc.sync.dma_start(lift_table[:, 0:U], lift)
         nc.sync.dma_start(tab_list[:], offs)
+        nc.sync.dma_start(lift_table[:, 0:U], lift)
         nc.sync.dma_start(w1_raw[:], w1.rearrange("(p t) r -> p t r", t=PACK))
         nc.sync.dma_start(word_table[:], tab_words[0].rearrange("p n t -> p (n t)").bitcast(I32))
         nc.sync.dma_start(dy_raw[:], dy.rearrange("(p t) m -> p t m", t=PACK))
@@ -64,18 +64,16 @@ def tile_attend_cliftedpicks_kernel(tc, tab_words, tab_scales, w1, lift, wo, dy,
         nc.sync.dma_start(pick_lists[:], offs3)
         nc.sync.dma_start(old_sb[:], old)
 
-        nc.vector.memset(minus_one[:], -1.0)
-        warm = sb.tile([P, 1], F32)
-        nc.scalar.activation(warm[:], minus_one[:], ACT.Exp)
+        one = sb.tile([P, 1], F32)
+        nc.vector.memset(one[:], 1.0)
+        nc.scalar.activation(minus_one[:], one[:], ACT.Copy, scale=-1.0)
         nc.vector.memset(lift_table[:, U:LIFT_WINDOW], 0.0)
         nc.vector.memset(s1[:], 0.0)
 
         e_lift = sb.tile([P, J], F32)
         e_lift2 = sb.tile([P, J], F32)
         nc.scalar.activation(e_lift[:], lift_table[:].indirect(lift_list[:]), ACT.Exp)
-
-        tab_sc = sb.tile([P, J], U8, align_bytes=64)
-        nc.vector.tensor_copy(tab_sc[:], scale_table[:].indirect(tab_list[:]))
+        nc.scalar.activation(e_lift2[:], e_lift[:], ACT.Copy, scale=2.0)
 
         w1_bf = sb.tile([P, R, PACK], BF16, align_bytes=64)
         wo_bf = sb.tile([P, R, PACK], BF16, align_bytes=64)
@@ -88,7 +86,8 @@ def tile_attend_cliftedpicks_kernel(tc, tab_words, tab_scales, w1, lift, wo, dy,
         dy_sc = sb.tile([P, M], U8, align_bytes=64)
         interleave(nc.vector.tensor_copy, w1_bf[:], w1_raw[:])
         quantize(nc, w1_codes, w1_sc, w1_bf)
-        nc.vector.tensor_scalar(e_lift2[:], e_lift[:], 2.0, None, ALU.mult)
+        tab_sc = sb.tile([P, J], U8, align_bytes=64)
+        nc.vector.tensor_copy(tab_sc[:], scale_table[:].indirect(tab_list[:]))
 
         h2 = sb.tile([P, J], F32, tag="h2")
         sig2a = sb.tile([P, J], F32)

from contextlib import ExitStack

import concourse.mybir as mybir

F32 = mybir.dt.float32
BF16 = mybir.dt.bfloat16
I32 = mybir.dt.int32
U32 = mybir.dt.uint32
U16 = mybir.dt.uint16
U8 = mybir.dt.uint8
FP8X4 = mybir.dt.float8_e4m3fn_x4
ACT = mybir.ActivationFunctionType
ALU = mybir.AluOpType

P = 128
PACK = 4
K, R, F, T, J, U, M = 512, 128, 512, 2048, 512, 1024, 256
HALF = J // 2
LIFT_WINDOW = 2048

FLOPS = 2 * K * R * J + 2 * F * R * M


def quantize(nc, codes, scales, grouped):
    nc.vector.quantize_mx(out=codes[:].bitcast(FP8X4), scales=scales[:], in_=grouped[:].rearrange("p c t -> p (c t)"))


def interleave(copy, grouped, raw):
    copy(
        out=grouped.rearrange("p (c i) t -> p c t i", i=4),
        in_=raw.rearrange("p t (c i) -> p c t i", i=4),
    )


def tile_attend_cliftedpicks_kernel(tc, tab_words, tab_scales, w1, lift, wo, dy, old, offs, offs2, offs3, out):
    nc = tc.nc
    with ExitStack() as ctx:
        sb = ctx.enter_context(tc.tile_pool(name="sb", bufs=1))
        ps = ctx.enter_context(tc.psum_pool(name="ps", bufs=1))

        tab_list = sb.tile([P, J // 16], U16)
        lift_list = sb.tile([P, J // 16], U16)
        pick_lists = sb.tile([P, M // 16], U16)
        scale_table = sb.tile([P, T], U8, align_bytes=64)
        lift_table = sb.tile([P, LIFT_WINDOW], F32)
        word_table = sb.tile([P, T], I32, align_bytes=64)
        w1_raw = sb.tile([P, PACK, R], F32)
        wo_raw = sb.tile([P, PACK, R], F32)
        dy_raw = sb.tile([P, PACK, M], F32)
        old_sb = sb.tile([P, J], F32)
        s1 = sb.tile([P, J], F32)
        minus_one = sb.tile([P, 1], F32)

        nc.vector.memset(scale_table[:].bitcast(I32), 0)
        for q in range(4):
            nc.scalar.dma_start(scale_table[32 * q : 32 * q + 4, :].bitcast(I32), tab_scales[0, 4 * q : 4 * q + 4, :].bitcast(I32))
        nc.sync.dma_start(lift_list[:], offs2)
        nc.sync.dma_start(tab_list[:], offs)
        nc.sync.dma_start(lift_table[:, 0:U], lift)
        nc.sync.dma_start(w1_raw[:], w1.rearrange("(p t) r -> p t r", t=PACK))
        nc.sync.dma_start(word_table[:], tab_words[0].rearrange("p n t -> p (n t)").bitcast(I32))
        nc.sync.dma_start(dy_raw[:], dy.rearrange("(p t) m -> p t m", t=PACK))
        nc.sync.dma_start(wo_raw[:], wo.rearrange("(p t) r -> p t r", t=PACK))
        nc.sync.dma_start(pick_lists[:], offs3)
        nc.sync.dma_start(old_sb[:], old)

        one = sb.tile([P, 1], F32)
        nc.vector.memset(one[:], 1.0)
        nc.scalar.activation(minus_one[:], one[:], ACT.Copy, scale=-1.0)
        nc.vector.memset(lift_table[:, U:LIFT_WINDOW], 0.0)
        nc.vector.memset(s1[:], 0.0)

        e_lift = sb.tile([P, J], F32)
        e_lift2 = sb.tile([P, J], F32)
        nc.scalar.activation(e_lift[:], lift_table[:].indirect(lift_list[:]), ACT.Exp)
        nc.scalar.activation(e_lift2[:], e_lift[:], ACT.Copy, scale=2.0)

        w1_bf = sb.tile([P, R, PACK], BF16, align_bytes=64)
        wo_bf = sb.tile([P, R, PACK], BF16, align_bytes=64)
        dy_bf = sb.tile([P, M, PACK], BF16, align_bytes=64)
        w1_codes = sb.tile([P, R], U32, align_bytes=64)
        w1_sc = sb.tile([P, R], U8, align_bytes=64)
        wo_codes = sb.tile([P, R], U32, align_bytes=64)
        wo_sc = sb.tile([P, R], U8, align_bytes=64)
        dy_codes = sb.tile([P, M], U32, align_bytes=64)
        dy_sc = sb.tile([P, M], U8, align_bytes=64)
        interleave(nc.vector.tensor_copy, w1_bf[:], w1_raw[:])
        quantize(nc, w1_codes, w1_sc, w1_bf)
        tab_sc = sb.tile([P, J], U8, align_bytes=64)
        nc.vector.tensor_copy(tab_sc[:], scale_table[:].indirect(tab_list[:]))

        h2 = sb.tile([P, J], F32, tag="h2")
        sig2a = sb.tile([P, J], F32)
        halves = [slice(0, HALF), slice(HALF, J)]
        a_ps = []
        for h in range(2):
            words = sb.tile([P, HALF], U32, align_bytes=64, name="words%d" % h)
            nc.vector.tensor_copy(words[:], word_table[:].bitcast(U32).indirect(tab_list[:, 16 * h : 16 * (h + 1)]))
            bank = ps.tile([P, HALF], F32, name="a%d" % h)
            nc.tensor.matmul_mx(
                out=bank[:], lhsT=w1_codes[:].bitcast(FP8X4), lhsT_scale=w1_sc[:],
                rhs=words[:].bitcast(FP8X4), rhs_scale=tab_sc[:, halves[h]], start=True, stop=True,
            )
            a_ps.append(bank)

        def lifted(h):
            c = halves[h]
            nc.scalar.activation(sig2a[:, c], a_ps[h][:], ACT.Sigmoid, scale=2.0)
            nc.vector.scalar_tensor_tensor(h2[:, c], sig2a[:, c], 0.5, e_lift2[:, c], ALU.subtract, ALU.mult)

        interleave(nc.vector.tensor_copy, dy_bf[:], dy_raw[:])
        lifted(0)
        quantize(nc, dy_codes, dy_sc, dy_bf)
        interleave(nc.scalar.copy, wo_bf[:, 0 : R // 2, :], wo_raw[:, :, 0 : R // 2])
        lifted(1)
        interleave(nc.scalar.copy, wo_bf[:, R // 2 : R, :], wo_raw[:, :, R // 2 : R])
        quantize(nc, wo_codes, wo_sc, wo_bf)
        c0_ps = ps.tile([P, M], F32)
        nc.tensor.matmul_mx(
            out=c0_ps[:], lhsT=wo_codes[:].bitcast(FP8X4), lhsT_scale=wo_sc[:],
            rhs=dy_codes[:].bitcast(FP8X4), rhs_scale=dy_sc[:], start=True, stop=True,
        )

        x = sb.tile([P, M], F32)
        s = sb.tile([P, M], F32)
        v = sb.tile([P, M], F32)
        d = sb.tile([P, M], F32)
        picks = [slice(0, M // 2), slice(M // 2, M)]
        for h in range(2):
            lists = pick_lists[:, 8 * h : 8 * (h + 1)]
            nc.scalar.activation(s[:, picks[h]], h2[:].indirect(lists), ACT.Sigmoid)
            nc.vector.tensor_copy(x[:, picks[h]], h2[:].indirect(lists))
        late = sb.tile([P, M + HALF], F32, tag="h2")
        c0_neg = late[:, 0:M]
        nc.scalar.activation(c0_neg, c0_ps[:], ACT.Copy, scale=-1.0)
        for c in picks:
            nc.vector.scalar_tensor_tensor(v[:, c], s[:, c], 1.0, x[:, c], ALU.subtract, ALU.mult)
        for c in picks:
            nc.vector.scalar_tensor_tensor(d[:, c], v[:, c], 1.0, s[:, c], ALU.subtract, ALU.mult)
        nc.vector.tensor_tensor(s1[:].indirect(pick_lists[:]), d[:], c0_neg, ALU.mult)

        h1_sq0 = sb.tile([P, HALF], F32)
        h1_sq = [h1_sq0[:], late[:, M : M + HALF]]
        slope_neg = sb.tile([P, J], F32)
        for h, c in enumerate(halves):
            nc.scalar.activation(h1_sq[h], sig2a[:, c], ACT.Square, scale=2.0, bias=minus_one[:])
            nc.vector.scalar_tensor_tensor(slope_neg[:, c], h1_sq[h], 1.0, e_lift[:, c], ALU.subtract, ALU.mult)

        da_neg = sb.tile([P, J], F32)
        y = sb.tile([P, J], F32)
        for c in halves:
            nc.vector.tensor_tensor(da_neg[:, c], s1[:, c], slope_neg[:, c], ALU.mult)
        for c in halves:
            nc.vector.tensor_tensor(y[:, c], old_sb[:, c], da_neg[:, c], ALU.subtract)
            nc.sync.dma_start(out[:, c], y[:, c])
